import numpy as np
import ml_dtypes


def mxq(x, axis, fmt="e4m3"):
    dtype, down = {"e4m3": (ml_dtypes.float8_e4m3fn, 7), "e5m2": (ml_dtypes.float8_e5m2, 14)}[fmt]
    v = np.moveaxis(np.asarray(x, np.float32).astype(ml_dtypes.bfloat16).astype(np.float64), axis, -1)
    blocks = v.reshape(v.shape[:-1] + (-1, 32))
    amax = np.abs(blocks).max(-1, keepdims=True)
    byte = np.maximum(np.where(amax > 0, np.frexp(amax)[1] - 1 + 127, 0) - down, 1)
    scale = np.exp2(byte - 127.0)
    codes = (blocks / scale).astype(np.float32).astype(dtype).astype(np.float64)
    return np.moveaxis((codes * scale).reshape(v.shape), -1, axis)


WIDE = False


def mx_kscale(k):
    if not WIDE:
        return np.ones(k)
    levels = np.array([10, -10, 5, -5, 0])
    if k % 512:
        return np.exp2(np.random.permutation(np.resize(levels, k // 32))).repeat(32)
    a = np.empty((k // 512, 16))
    for p in range(k // 512):
        a[p, :8] = np.random.permutation(np.resize(levels, 8))
        for g in range(8):
            far = levels[np.abs(levels - a[p, g]) >= 10]
            a[p, g + 8] = far[np.random.randint(len(far))]
    return np.exp2(a.ravel()).repeat(32)


def f64(x):
    return np.asarray(x).astype(np.float64)


def striped(idx):
    return np.tile(idx.reshape(-1, 16).T, (8, 1)).astype(np.uint16)


def unstriped(offs):
    return offs[:16].T.reshape(-1).astype(np.int64)


def striped8(idx):
    return np.concatenate([x.reshape(-1, 16).T for x in idx]).astype(np.uint16)


def runs(offs, k):
    lists = np.stack([offs[16 * r : 16 * r + 16].T.reshape(-1) for r in range(8)]).astype(np.int64)
    return lists[np.arange(k) % 512 // 64]


def pack_weight(w):
    k, n = w.shape
    w = f64(np.asarray(w, np.float32).astype(ml_dtypes.bfloat16)).reshape(k // 32, 32, n)
    amax = np.abs(w).max(1)
    byte = np.clip(np.where(amax > 0, np.frexp(amax)[1] - 1 + 127 - 7, 1), 1, 254)
    scaled = (w * np.exp2(127.0 - byte)[:, None, :]).reshape(k, n).astype(np.float32)
    words = np.ascontiguousarray(scaled.reshape(k // 512, 128, 4, n).transpose(0, 1, 3, 2)).astype(ml_dtypes.float8_e4m3fn).view(np.uint8)
    return words, np.ascontiguousarray(byte.astype(np.uint8).reshape(k // 512, 16, n))


def unpack_weight(words, scales):
    g, p, n, _ = words.shape
    vals = np.ascontiguousarray(words).view(ml_dtypes.float8_e4m3fn).astype(np.float64) * np.repeat(np.exp2(scales.astype(np.float64) - 127.0), 8, axis=1)[..., None]
    return vals.transpose(0, 1, 3, 2).reshape(g * 512, n)


K, T, S, H, C = 512, 2048, 512, 512, 512


def setup_inputs():
    n = np.random.standard_normal
    s = mx_kscale(K)[:, None]
    packed_xT = pack_weight(n((K, T)) * s)
    return {
        "x_words": packed_xT[0],
        "x_scales": packed_xT[1],
        "w1": (n((K, H)) / np.sqrt(K) / s).astype(np.float32),
        "gs": (np.random.uniform(0.5, 1.5, (K, 1)) / s).astype(np.float32),
        "offs": striped(np.random.permutation(T)[:S]),
        "n1": striped8(np.stack([np.random.permutation(S) for _ in range(8)])),
        "ca": striped(np.random.permutation(T)[:C]),
        "cb": striped(np.random.permutation(T)[:C]),
        "n2": striped8(np.stack([np.random.permutation(S) for _ in range(8)])),
        "n3": striped8(np.stack([np.random.permutation(S) for _ in range(8)])),
    }


def reference(x_words, x_scales, w1, gs, offs, n1, ca, cb, n2, n3):
    x_ca = unpack_weight(x_words, x_scales)[:, unstriped(ca)]
    xq = unpack_weight(x_words, x_scales)[:, unstriped(offs)]
    y = mxq(f64(w1), 0, "e4m3").T @ xq
    z = f64(gs) * (y - (y[np.arange(H)[:, None], runs(n1, H)]))
    zq = mxq(z, 0, "e4m3")
    a = 0.0625 * (x_ca.T @ zq)
    x_cb = unpack_weight(x_words, x_scales)[:, unstriped(cb)]
    b = 0.0625 * (x_cb.T @ zq)
    return (a - (a[np.arange(C)[:, None], runs(n2, C)])) / (np.abs(b) + np.abs(b[np.arange(C)[:, None], runs(n3, C)]) + 0.5)

@@ -1,0 +1,178 @@
+from contextlib import ExitStack
+
+import concourse.mybir as mybir
+
+K, T, S, H, C = 512, 2048, 512, 512, 512
+FLOPS = 2 * K * H * S + 2 * 2 * K * C * S
+
+F32 = mybir.dt.float32
+BF16 = mybir.dt.bfloat16
+I32 = mybir.dt.int32
+U32 = mybir.dt.uint32
+U16 = mybir.dt.uint16
+U8 = mybir.dt.uint8
+FP8X4 = mybir.dt.float8_e4m3fn_x4
+ACT = mybir.ActivationFunctionType
+ALU = mybir.AluOpType
+
+P = 128
+PACK = 4
+HALF = S // 2
+RUN = 8
+SIXTEENTH = 0.0625
+
+
+def tile_picked_ccmpnormbdif_none_p_kernel(
+    tc, x_words, x_scales, w1, gs, offs, n1, ca, cb, n2, n3, out
+):
+    nc = tc.nc
+    with ExitStack() as ctx:
+        held = ctx.enter_context(tc.tile_pool(name="held", bufs=1))
+        psum = ctx.enter_context(tc.psum_pool(name="psum", bufs=1))
+
+        def load_list(name, src):
+            tile = held.tile([P, S // 16], U16, name=name)
+            nc.sync.dma_start(tile[:], src)
+            return tile
+
+        table_scales = held.tile([P, T], U8, name="table_scales", align_bytes=64)
+        nc.vector.memset(table_scales[:].bitcast(I32), 0)
+        offs_list = load_list("offs_list", offs)
+        cb_list = load_list("cb_list", cb)
+        for q in range(4):
+            nc.sync.dma_start(
+                table_scales[32 * q : 32 * q + 4, :].bitcast(I32),
+                x_scales[0, 4 * q : 4 * q + 4, :].bitcast(I32),
+            )
+        w_rows = w1.rearrange("(p j) h -> p j h", j=PACK)
+        w_raw = []
+        for u in range(2):
+            part = held.tile([P, PACK, H // 2], F32, name="w_raw%d" % u)
+            nc.sync.dma_start(part[:], w_rows[:, :, u * (H // 2) : (u + 1) * (H // 2)])
+            w_raw.append(part)
+        table_words = held.tile([P, T], U32, name="table_words", align_bytes=64)
+        nc.sync.dma_start(
+            table_words[:].bitcast(I32),
+            x_words[0].rearrange("p n t -> p (n t)").bitcast(I32),
+        )
+        ca_list = load_list("ca_list", ca)
+        n1_list = load_list("n1_list", n1)
+        n3_list = load_list("n3_list", n3)
+        n2_list = load_list("n2_list", n2)
+        gain = held.tile([P, PACK], F32, name="gain")
+        nc.gpsimd.dma_start(gain[:], gs.rearrange("(p t) o -> p (t o)", t=PACK))
+
+        tok_scales = held.tile([P, S], U8, name="tok_scales", align_bytes=64)
+        nc.vector.tensor_copy(tok_scales[:], table_scales[:].indirect(offs_list[:]))
+
+        def pick_scales(name, lst):
+            raw = held.tile([P, C], U8, name=name + "_raw", align_bytes=64)
+            nc.vector.tensor_copy(raw[:], table_scales[:].indirect(lst[:]))
+            dealt = held.tile([P, C], U8, name=name, align_bytes=64)
+            nc.vector.tensor_copy(
+                dealt[:].bitcast(I32).rearrange("p (t q w) -> p t q w", t=PACK, w=RUN // 4),
+                raw[:].bitcast(I32).rearrange("p (q t w) -> p t q w", t=PACK, w=RUN // 4),
+            )
+            return dealt
+
+        def pick_words(name, lst):
+            dealt = held.tile([P, C], U32, name=name, align_bytes=64)
+            nc.vector.tensor_copy(
+                dealt[:].rearrange("p (t q r) -> p q t r", t=PACK, r=RUN),
+                table_words[:].indirect(lst[:]),
+            )
+            return dealt
+
+        cb_scales = pick_scales("cb_scales", cb_list)
+
+        w_bf = held.tile([P, PACK, P, PACK], BF16, name="w_bf", align_bytes=64)
+        for u in range(2):
+            nc.scalar.copy(
+                w_bf[:, :, u * 64 : (u + 1) * 64, :].rearrange("p t m j -> p m j t"),
+                w_raw[u][:].rearrange("p j (m t) -> p m j t", t=PACK),
+            )
+        w_codes = held.tile([P, H], U32, name="w_codes", align_bytes=64)
+        w_scales = held.tile([P, H], U8, name="w_scales", align_bytes=64)
+        nc.vector.quantize_mx(
+            out=w_codes[:].bitcast(FP8X4),
+            scales=w_scales[:],
+            in_=w_bf[:].rearrange("p t m j -> p (t m j)"),
+        )
+
+        tok_words = held.tile([P, S], U32, name="tok_words", align_bytes=64)
+        nc.vector.tensor_copy(tok_words[:], table_words[:].indirect(offs_list[:]))
+        cb_words = pick_words("cb_words", cb_list)
+
+        def product(bank, codes, scales, t, rhs, rhs_scale):
+            acc = psum.tile([P, S], F32, name="bank%d" % bank)
+            cols = slice(t * P, (t + 1) * P)
+            nc.tensor.matmul_mx(
+                out=acc[:],
+                lhsT=codes[:, cols].bitcast(FP8X4),
+                lhsT_scale=scales[:, cols],
+                rhs=rhs[:].bitcast(FP8X4),
+                rhs_scale=rhs_scale[:],
+                start=True,
+                stop=True,
+            )
+            return acc
+
+        def twice(name, acc, func, scale):
+            window = held.tile([P, S], F32, name=name + "_window")
+            plain = held.tile([P, S], F32, name=name + "_plain")
+            nc.scalar.activation(window[:], acc[:], func, scale=scale)
+            nc.scalar.activation(plain[:], acc[:], func, scale=scale)
+            return window, plain
+
+        def fetch(dst, window, plain, lst, h, op):
+            nc.vector.tensor_tensor(
+                dst,
+                window[:].indirect(lst[:, h * 16 : (h + 1) * 16]),
+                plain[:, h * HALF : (h + 1) * HALF],
+                op,
+            )
+
+        neg_z = [held.tile([P, PACK, HALF], F32, name="neg_z%d" % h) for h in range(2)]
+        for t in range(PACK):
+            acc = product(t, w_codes, w_scales, t, tok_words, tok_scales)
+            window, plain = twice("y%d" % t, acc, ACT.Copy, gain[:, t : t + 1])
+            for h in range(2):
+                fetch(neg_z[h][:, t, :], window, plain, n1_list, h, ALU.subtract)
+
+        z_codes = held.tile([P, S], U32, name="z_codes", align_bytes=64)
+        z_scales = held.tile([P, S], U8, name="z_scales", align_bytes=64)
+        z_bf = [held.tile([P, HALF * PACK], BF16, name="z_bf%d" % h, align_bytes=64) for h in range(2)]
+        for h, copy in ((0, nc.scalar.copy), (1, nc.vector.tensor_copy)):
+            copy(
+                z_bf[h][:].rearrange("p (c i t) -> p c t i", i=4, t=PACK),
+                neg_z[h][:].rearrange("p t (c i) -> p c t i", i=4),
+            )
+        for h in range(2):
+            nc.vector.quantize_mx(
+                out=z_codes[:, h * HALF : (h + 1) * HALF].bitcast(FP8X4),
+                scales=z_scales[:, h * HALF : (h + 1) * HALF],
+                in_=z_bf[h][:],
+            )
+
+        ca_scales = pick_scales("ca_scales", ca_list)
+        ca_words = pick_words("ca_words", ca_list)
+
+        out_rows = out.rearrange("(q t r) j -> t q r j", t=PACK, r=RUN)
+        for t in range(PACK):
+            acc_b = product(4 + t, cb_words, cb_scales, t, z_codes, z_scales)
+            acc_a = product(t, ca_words, ca_scales, t, z_codes, z_scales)
+            b_window, b_plain = twice("b%d" % t, acc_b, ACT.Abs, SIXTEENTH)
+            a_window, a_plain = twice("a%d" % t, acc_a, ACT.Copy, SIXTEENTH)
+            sizes = held.tile([P, S], F32, name="sizes%d" % t)
+            diff = held.tile([P, S], F32, name="diff%d" % t)
+            for h in range(2):
+                fetch(sizes[:, h * HALF : (h + 1) * HALF], b_window, b_plain, n3_list, h, ALU.add)
+            for h in range(2):
+                fetch(diff[:, h * HALF : (h + 1) * HALF], a_window, a_plain, n2_list, h, ALU.subtract)
+            root = held.tile([P, S], F32, name="root%d" % t)
+            nc.scalar.activation(root[:], sizes[:], ACT.Abs_reciprocal_sqrt, bias=0.5)
+            recip = held.tile([P, S], F32, name="recip%d" % t)
+            nc.scalar.activation(recip[:], root[:], ACT.Square)
+            result = held.tile([P, S], F32, name="result%d" % t)
+            nc.vector.tensor_tensor(result[:], diff[:], recip[:], ALU.mult)
+            nc.sync.dma_start(out_rows[t], result[:])

@@ -37,13 +37,18 @@ def tile_picked_ccmpnormbdif_none_p_kernel(
 
         table_scales = held.tile([P, T], U8, name="table_scales", align_bytes=64)
         nc.vector.memset(table_scales[:].bitcast(I32), 0)
-        offs_list = load_list("offs_list", offs)
-        cb_list = load_list("cb_list", cb)
         for q in range(4):
             nc.sync.dma_start(
                 table_scales[32 * q : 32 * q + 4, :].bitcast(I32),
                 x_scales[0, 4 * q : 4 * q + 4, :].bitcast(I32),
             )
+        warm_in = held.tile([P, 1], F32, name="warm_in")
+        warm_out = held.tile([P, 1], F32, name="warm_out")
+        nc.vector.memset(warm_in[:], 1.0)
+        nc.scalar.activation(warm_out[:], warm_in[:], ACT.Abs_reciprocal_sqrt, bias=0.5)
+        offs_list = load_list("offs_list", offs)
+        cb_list = load_list("cb_list", cb)
+        ca_list = load_list("ca_list", ca)
         w_rows = w1.rearrange("(p j) h -> p j h", j=PACK)
         w_raw = []
         for u in range(2):
@@ -55,12 +60,11 @@ def tile_picked_ccmpnormbdif_none_p_kernel(
             table_words[:].bitcast(I32),
             x_words[0].rearrange("p n t -> p (n t)").bitcast(I32),
         )
-        ca_list = load_list("ca_list", ca)
         n1_list = load_list("n1_list", n1)
+        gain = held.tile([P, PACK], F32, name="gain")
+        nc.sync.dma_start(gain[:], gs.rearrange("(p t) o -> p (t o)", t=PACK))
         n3_list = load_list("n3_list", n3)
         n2_list = load_list("n2_list", n2)
-        gain = held.tile([P, PACK], F32, name="gain")
-        nc.gpsimd.dma_start(gain[:], gs.rearrange("(p t) o -> p (t o)", t=PACK))
 
         tok_scales = held.tile([P, S], U8, name="tok_scales", align_bytes=64)
         nc.vector.tensor_copy(tok_scales[:], table_scales[:].indirect(offs_list[:]))
@@ -75,8 +79,8 @@ def tile_picked_ccmpnormbdif_none_p_kernel(
             )
             return dealt
 
-        def pick_words(name, lst):
-            dealt = held.tile([P, C], U32, name=name, align_bytes=64)
+        def pick_words(name, lst, tag):
+            dealt = held.tile([P, C], U32, name=name, tag=tag, align_bytes=64)
             nc.vector.tensor_copy(
                 dealt[:].rearrange("p (t q r) -> p q t r", t=PACK, r=RUN),
                 table_words[:].indirect(lst[:]),
@@ -84,6 +88,7 @@ def tile_picked_ccmpnormbdif_none_p_kernel(
             return dealt
 
         cb_scales = pick_scales("cb_scales", cb_list)
+        ca_scales = pick_scales("ca_scales", ca_list)
 
         w_bf = held.tile([P, PACK, P, PACK], BF16, name="w_bf", align_bytes=64)
         for u in range(2):
@@ -101,7 +106,7 @@ def tile_picked_ccmpnormbdif_none_p_kernel(
 
         tok_words = held.tile([P, S], U32, name="tok_words", align_bytes=64)
         nc.vector.tensor_copy(tok_words[:], table_words[:].indirect(offs_list[:]))
-        cb_words = pick_words("cb_words", cb_list)
+        cb_words = pick_words("cb_words", cb_list, "cb_words")
 
         def product(bank, codes, scales, t, rhs, rhs_scale):
             acc = psum.tile([P, S], F32, name="bank%d" % bank)
@@ -117,35 +122,47 @@ def tile_picked_ccmpnormbdif_none_p_kernel(
             )
             return acc
 
-        def twice(name, acc, func, scale):
-            window = held.tile([P, S], F32, name=name + "_window")
-            plain = held.tile([P, S], F32, name=name + "_plain")
-            nc.scalar.activation(window[:], acc[:], func, scale=scale)
-            nc.scalar.activation(plain[:], acc[:], func, scale=scale)
+        wide = [held.tile([P, 2 * S], F32, name="wide%d" % i) for i in range(3 * PACK)]
+        first_window = held.tile([P, S], F32, name="first_window")
+        windows = [first_window] + wide
+        taken = []
+
+        def twice(acc, func, scale, on_vector):
+            i = len(taken)
+            taken.append(i)
+            window = windows[i]
+            plain = windows[i + 1][:, S:]
+            nc.scalar.activation(window[:, :S], acc[:], func, scale=scale)
+            if on_vector:
+                nc.vector.tensor_copy(plain, window[:, :S])
+            else:
+                nc.scalar.activation(plain, acc[:], func, scale=scale)
             return window, plain
 
-        def fetch(dst, window, plain, lst, h, op):
-            nc.vector.tensor_tensor(
-                dst,
-                window[:].indirect(lst[:, h * 16 : (h + 1) * 16]),
-                plain[:, h * HALF : (h + 1) * HALF],
-                op,
-            )
+        def fetch(dst, window, plain, lst, op, pieces):
+            width = S // pieces
+            for h in range(pieces):
+                cols = slice(h * width, (h + 1) * width)
+                nc.vector.tensor_tensor(
+                    dst[:, cols],
+                    window[:].indirect(lst[:, h * width // 16 : (h + 1) * width // 16]),
+                    plain[:, cols],
+                    op,
+                )
 
-        neg_z = [held.tile([P, PACK, HALF], F32, name="neg_z%d" % h) for h in range(2)]
+        neg_z = held.tile([P, PACK, S], F32, name="neg_z")
         for t in range(PACK):
             acc = product(t, w_codes, w_scales, t, tok_words, tok_scales)
-            window, plain = twice("y%d" % t, acc, ACT.Copy, gain[:, t : t + 1])
-            for h in range(2):
-                fetch(neg_z[h][:, t, :], window, plain, n1_list, h, ALU.subtract)
+            window, plain = twice(acc, ACT.Copy, gain[:, t : t + 1], t == 0)
+            fetch(neg_z[:, t, :], window, plain, n1_list, ALU.subtract, 2 if t in (0, PACK - 1) else 1)
 
         z_codes = held.tile([P, S], U32, name="z_codes", align_bytes=64)
         z_scales = held.tile([P, S], U8, name="z_scales", align_bytes=64)
-        z_bf = [held.tile([P, HALF * PACK], BF16, name="z_bf%d" % h, align_bytes=64) for h in range(2)]
+        z_bf = [held.tile([P, HALF * PACK], BF16, name="z_bf%d" % h, tag="z_bf%d" % h, align_bytes=64) for h in range(2)]
         for h, copy in ((0, nc.scalar.copy), (1, nc.vector.tensor_copy)):
             copy(
                 z_bf[h][:].rearrange("p (c i t) -> p c t i", i=4, t=PACK),
-                neg_z[h][:].rearrange("p t (c i) -> p c t i", i=4),
+                neg_z[:, :, h * HALF : (h + 1) * HALF].rearrange("p t (c i) -> p c t i", i=4),
             )
         for h in range(2):
             nc.vector.quantize_mx(
@@ -154,25 +171,41 @@ def tile_picked_ccmpnormbdif_none_p_kernel(
                 in_=z_bf[h][:],
             )
 
-        ca_scales = pick_scales("ca_scales", ca_list)
-        ca_words = pick_words("ca_words", ca_list)
+        ca_words = pick_words("ca_words", ca_list, "z_bf0")
 
         out_rows = out.rearrange("(q t r) j -> t q r j", t=PACK, r=RUN)
-        for t in range(PACK):
-            acc_b = product(4 + t, cb_words, cb_scales, t, z_codes, z_scales)
-            acc_a = product(t, ca_words, ca_scales, t, z_codes, z_scales)
-            b_window, b_plain = twice("b%d" % t, acc_b, ACT.Abs, SIXTEENTH)
-            a_window, a_plain = twice("a%d" % t, acc_a, ACT.Copy, SIXTEENTH)
-            sizes = held.tile([P, S], F32, name="sizes%d" % t)
-            diff = held.tile([P, S], F32, name="diff%d" % t)
-            for h in range(2):
-                fetch(sizes[:, h * HALF : (h + 1) * HALF], b_window, b_plain, n3_list, h, ALU.add)
-            for h in range(2):
-                fetch(diff[:, h * HALF : (h + 1) * HALF], a_window, a_plain, n2_list, h, ALU.subtract)
+        sizes, diffs, recips = {}, {}, {}
+
+        def b_side(t):
+            acc = product(4 + t, cb_words, cb_scales, t, z_codes, z_scales)
+            window, plain = twice(acc, ACT.Abs, SIXTEENTH, t % 2 == 0)
+            sizes[t] = held.tile([P, S], F32, name="sizes%d" % t)
+            fetch(sizes[t], window, plain, n3_list, ALU.add, 1)
+
+        def a_side(t):
+            acc = product(t, ca_words, ca_scales, t, z_codes, z_scales)
+            window, plain = twice(acc, ACT.Copy, SIXTEENTH, False)
+            diffs[t] = held.tile([P, S], F32, name="diff%d" % t)
+            fetch(diffs[t], window, plain, n2_list, ALU.subtract, 2 if t == PACK - 1 else 1)
+
+        def invert(t):
             root = held.tile([P, S], F32, name="root%d" % t)
-            nc.scalar.activation(root[:], sizes[:], ACT.Abs_reciprocal_sqrt, bias=0.5)
-            recip = held.tile([P, S], F32, name="recip%d" % t)
-            nc.scalar.activation(recip[:], root[:], ACT.Square)
-            result = held.tile([P, S], F32, name="result%d" % t)
-            nc.vector.tensor_tensor(result[:], diff[:], recip[:], ALU.mult)
-            nc.sync.dma_start(out_rows[t], result[:])
+            nc.scalar.activation(root[:], sizes[t][:], ACT.Abs_reciprocal_sqrt, bias=0.5)
+            recips[t] = held.tile([P, S], F32, name="recip%d" % t)
+            nc.scalar.activation(recips[t][:], root[:], ACT.Square)
+
+        def finish(t, pieces):
+            width = S // pieces
+            for h in range(pieces):
+                cols = slice(h * width, (h + 1) * width)
+                result = held.tile([P, width], F32, name="result%d_%d" % (t, h))
+                nc.vector.tensor_tensor(result[:], diffs[t][:, cols], recips[t][:, cols], ALU.mult)
+                nc.sync.dma_start(out_rows[t][:, :, cols], result[:])
+
+        b_side(0)
+        for t in range(PACK):
+            if t + 1 < PACK:
+                b_side(t + 1)
+            a_side(t)
+            invert(t)
+            finish(t, 2 if t == PACK - 1 else 1)

@@ -1,6 +1,7 @@
 from contextlib import ExitStack
 
 import concourse.mybir as mybir
+from concourse.masks import make_identity
 
 K, T, S, H, C = 512, 2048, 512, 512, 512
 FLOPS = 2 * K * H * S + 2 * 2 * K * C * S
@@ -66,18 +67,23 @@ def tile_picked_ccmpnormbdif_none_p_kernel(
         n3_list = load_list("n3_list", n3)
         n2_list = load_list("n2_list", n2)
 
+        identity = held.tile([P, P], F32, name="identity")
+        nc.vector.memset(identity[:], 0.0)
+        make_identity(nc, identity[:], nomemset=True)
+        wide = [held.tile([P, 2 * S], F32, name="wide%d" % i) for i in range(2 * PACK + 1)]
+        nc.vector.memset(wide[0][:, S:], 0.0)
+
+        pair_raw = held.tile([P, 2 * C], U8, name="pair_raw", align_bytes=64)
+        nc.vector.tensor_copy(pair_raw[:, :C], table_scales[:].indirect(cb_list[:]))
+        nc.vector.tensor_copy(pair_raw[:, C:], table_scales[:].indirect(ca_list[:]))
         tok_scales = held.tile([P, S], U8, name="tok_scales", align_bytes=64)
         nc.vector.tensor_copy(tok_scales[:], table_scales[:].indirect(offs_list[:]))
-
-        def pick_scales(name, lst):
-            raw = held.tile([P, C], U8, name=name + "_raw", align_bytes=64)
-            nc.vector.tensor_copy(raw[:], table_scales[:].indirect(lst[:]))
-            dealt = held.tile([P, C], U8, name=name, align_bytes=64)
-            nc.vector.tensor_copy(
-                dealt[:].bitcast(I32).rearrange("p (t q w) -> p t q w", t=PACK, w=RUN // 4),
-                raw[:].bitcast(I32).rearrange("p (q t w) -> p t q w", t=PACK, w=RUN // 4),
-            )
-            return dealt
+        pair_scales = held.tile([P, 2 * C], U8, name="pair_scales", align_bytes=64)
+        nc.vector.tensor_copy(
+            pair_scales[:].bitcast(I32).rearrange("p (l t q w) -> p l t q w", l=2, t=PACK, w=RUN // 4),
+            pair_raw[:].bitcast(I32).rearrange("p (l q t w) -> p l t q w", l=2, t=PACK, w=RUN // 4),
+        )
+        cb_scales, ca_scales = pair_scales[:, :C], pair_scales[:, C:]
 
         def pick_words(name, lst, tag):
             dealt = held.tile([P, C], U32, name=name, tag=tag, align_bytes=64)
@@ -86,9 +92,6 @@ def tile_picked_ccmpnormbdif_none_p_kernel(
                 table_words[:].indirect(lst[:]),
             )
             return dealt
-
-        cb_scales = pick_scales("cb_scales", cb_list)
-        ca_scales = pick_scales("ca_scales", ca_list)
 
         w_bf = held.tile([P, PACK, P, PACK], BF16, name="w_bf", align_bytes=64)
         for u in range(2):
@@ -104,108 +107,119 @@ def tile_picked_ccmpnormbdif_none_p_kernel(
             in_=w_bf[:].rearrange("p t m j -> p (t m j)"),
         )
 
+        halves = [slice(0, HALF), slice(HALF, S)]
+        whole = [slice(0, S)]
         tok_words = held.tile([P, S], U32, name="tok_words", align_bytes=64)
-        nc.vector.tensor_copy(tok_words[:], table_words[:].indirect(offs_list[:]))
+        for cols in halves:
+            nc.vector.tensor_copy(
+                tok_words[:, cols],
+                table_words[:].indirect(offs_list[:, cols.start // 16 : cols.stop // 16]),
+            )
         cb_words = pick_words("cb_words", cb_list, "cb_words")
 
-        def product(bank, codes, scales, t, rhs, rhs_scale):
-            acc = psum.tile([P, S], F32, name="bank%d" % bank)
-            cols = slice(t * P, (t + 1) * P)
-            nc.tensor.matmul_mx(
-                out=acc[:],
-                lhsT=codes[:, cols].bitcast(FP8X4),
-                lhsT_scale=scales[:, cols],
-                rhs=rhs[:].bitcast(FP8X4),
-                rhs_scale=rhs_scale[:],
-                start=True,
-                stop=True,
-            )
-            return acc
+        def bank(n, width=S):
+            return psum.tile([P, width], F32, name="bank%d" % n)
 
-        wide = [held.tile([P, 2 * S], F32, name="wide%d" % i) for i in range(3 * PACK)]
-        first_window = held.tile([P, S], F32, name="first_window")
-        windows = [first_window] + wide
-        taken = []
-
-        def twice(acc, func, scale, on_vector):
-            i = len(taken)
-            taken.append(i)
-            window = windows[i]
-            plain = windows[i + 1][:, S:]
-            nc.scalar.activation(window[:, :S], acc[:], func, scale=scale)
-            if on_vector:
-                nc.vector.tensor_copy(plain, window[:, :S])
-            else:
-                nc.scalar.activation(plain, acc[:], func, scale=scale)
-            return window, plain
+        def product(codes, scales, t, rhs, rhs_scale, func, scale, pieces, banks, copies):
+            rows = slice(t * P, (t + 1) * P)
+            for cols, n in zip(pieces, banks):
+                acc = bank(n, cols.stop - cols.start)
+                nc.tensor.matmul_mx(
+                    out=acc[:],
+                    lhsT=codes[:, rows].bitcast(FP8X4),
+                    lhsT_scale=scales[:, rows],
+                    rhs=rhs[:, cols].bitcast(FP8X4),
+                    rhs_scale=rhs_scale[:, cols],
+                    start=True,
+                    stop=True,
+                )
+                for dst in copies:
+                    nc.scalar.activation(dst[:, cols], acc[:], func, scale=scale)
 
         def fetch(dst, window, plain, lst, op, pieces):
-            width = S // pieces
-            for h in range(pieces):
-                cols = slice(h * width, (h + 1) * width)
+            for cols in pieces:
                 nc.vector.tensor_tensor(
                     dst[:, cols],
-                    window[:].indirect(lst[:, h * width // 16 : (h + 1) * width // 16]),
+                    window[:].indirect(lst[:, cols.start // 16 : cols.stop // 16]),
                     plain[:, cols],
                     op,
                 )
 
-        neg_z = held.tile([P, PACK, S], F32, name="neg_z")
+        last = PACK - 1
+        neg_z = held.tile([P, PACK, S], F32, name="neg_z", tag="neg_z", align_bytes=64)
         for t in range(PACK):
-            acc = product(t, w_codes, w_scales, t, tok_words, tok_scales)
-            window, plain = twice(acc, ACT.Copy, gain[:, t : t + 1], t == 0)
-            fetch(neg_z[:, t, :], window, plain, n1_list, ALU.subtract, 2 if t in (0, PACK - 1) else 1)
+            window, plain = wide[t], wide[t + 1][:, S:]
+            product(
+                w_codes, w_scales, t, tok_words, tok_scales, ACT.Copy, gain[:, t : t + 1],
+                halves if t == 0 else whole, (0, 1) if t == 0 else (t + 1,), (window, plain),
+            )
+            fetch(neg_z[:, t, :], window, plain, n1_list, ALU.subtract, halves if t == last else whole)
 
         z_codes = held.tile([P, S], U32, name="z_codes", align_bytes=64)
         z_scales = held.tile([P, S], U8, name="z_scales", align_bytes=64)
-        z_bf = [held.tile([P, HALF * PACK], BF16, name="z_bf%d" % h, tag="z_bf%d" % h, align_bytes=64) for h in range(2)]
+        z_bf = [held.tile([P, HALF * PACK], BF16, name="z_bf%d" % h, align_bytes=64) for h in range(2)]
         for h, copy in ((0, nc.scalar.copy), (1, nc.vector.tensor_copy)):
             copy(
                 z_bf[h][:].rearrange("p (c i t) -> p c t i", i=4, t=PACK),
-                neg_z[:, :, h * HALF : (h + 1) * HALF].rearrange("p t (c i) -> p c t i", i=4),
+                neg_z[:, :, halves[h]].rearrange("p t (c i) -> p c t i", i=4),
             )
-        for h in range(2):
+        for h in (1, 0):
             nc.vector.quantize_mx(
-                out=z_codes[:, h * HALF : (h + 1) * HALF].bitcast(FP8X4),
-                scales=z_scales[:, h * HALF : (h + 1) * HALF],
+                out=z_codes[:, halves[h]].bitcast(FP8X4),
+                scales=z_scales[:, halves[h]],
                 in_=z_bf[h][:],
             )
 
-        ca_words = pick_words("ca_words", ca_list, "z_bf0")
+        ca_words = pick_words("ca_words", ca_list, "neg_z")
 
         out_rows = out.rearrange("(q t r) j -> t q r j", t=PACK, r=RUN)
-        sizes, diffs, recips = {}, {}, {}
+        blocks = [slice(c * P, (c + 1) * P) for c in range(S // P)]
+        b_windows = [wide[(t + PACK) % (PACK + 1)] for t in range(PACK)]
+        a_windows = [wide[last]] + wide[PACK + 1 :]
+        picked, diffs, roots = {}, {}, {}
 
-        def b_side(t):
-            acc = product(4 + t, cb_words, cb_scales, t, z_codes, z_scales)
-            window, plain = twice(acc, ACT.Abs, SIXTEENTH, t % 2 == 0)
-            sizes[t] = held.tile([P, S], F32, name="sizes%d" % t)
-            fetch(sizes[t], window, plain, n3_list, ALU.add, 1)
+        for t in range(PACK):
+            product(
+                cb_words, cb_scales, t, z_codes, z_scales, ACT.Abs, SIXTEENTH,
+                halves[::-1] if t == 0 else whole, (5, 6) if t == 0 else ((6 + t) % 8,), (b_windows[t],),
+            )
+            picked[t] = held.tile([P, S], F32, name="picked%d" % t)
+            nc.vector.tensor_copy(picked[t][:], b_windows[t][:].indirect(n3_list[:]))
 
         def a_side(t):
-            acc = product(t, ca_words, ca_scales, t, z_codes, z_scales)
-            window, plain = twice(acc, ACT.Copy, SIXTEENTH, False)
+            window, plain = a_windows[t], a_windows[t + 1][:, S:]
+            product(
+                ca_words, ca_scales, t, z_codes, z_scales, ACT.Copy, SIXTEENTH, whole,
+                (2 + t % 3,), (window, plain),
+            )
             diffs[t] = held.tile([P, S], F32, name="diff%d" % t)
-            fetch(diffs[t], window, plain, n2_list, ALU.subtract, 2 if t == PACK - 1 else 1)
+            fetch(diffs[t], window, plain, n2_list, ALU.subtract, whole)
 
-        def invert(t):
-            root = held.tile([P, S], F32, name="root%d" % t)
-            nc.scalar.activation(root[:], sizes[t][:], ACT.Abs_reciprocal_sqrt, bias=0.5)
-            recips[t] = held.tile([P, S], F32, name="recip%d" % t)
-            nc.scalar.activation(recips[t][:], root[:], ACT.Square)
+        def root(t):
+            total = bank(5 + t % 2)
+            terms = [(src, cols) for src in (b_windows[t], picked[t]) for cols in blocks]
+            for i, (src, cols) in enumerate(terms):
+                nc.tensor.matmul(
+                    total[:, cols], src[:, cols], identity[:],
+                    start=(i == 0), stop=(i == len(terms) - 1), is_transpose=True,
+                )
+            turned = held.tile([P, S], F32, name="turned%d" % t)
+            nc.scalar.activation(turned[:], total[:], ACT.Abs_reciprocal_sqrt, bias=0.5)
+            roots[t] = bank((7 + t % 2) % 8)
+            for cols in blocks:
+                nc.tensor.transpose(roots[t][:, cols], turned[:, cols], identity[:])
 
         def finish(t, pieces):
-            width = S // pieces
-            for h in range(pieces):
-                cols = slice(h * width, (h + 1) * width)
-                result = held.tile([P, width], F32, name="result%d_%d" % (t, h))
-                nc.vector.tensor_tensor(result[:], diffs[t][:, cols], recips[t][:, cols], ALU.mult)
-                nc.sync.dma_start(out_rows[t][:, :, cols], result[:])
+            recip = held.tile([P, S], F32, name="recip%d" % t)
+            result = held.tile([P, S], F32, name="result%d" % t)
+            nc.scalar.activation(recip[:], roots[t][:], ACT.Square)
+            for cols in pieces:
+                nc.vector.tensor_tensor(result[:, cols], diffs[t][:, cols], recip[:, cols], ALU.mult)
+                nc.sync.dma_start(out_rows[t][:, :, cols], result[:, cols])
 
-        b_side(0)
         for t in range(PACK):
-            if t + 1 < PACK:
-                b_side(t + 1)
             a_side(t)
-            invert(t)
-            finish(t, 2 if t == PACK - 1 else 1)
+            root(t)
+            if t > 0:
+                finish(t - 1, whole)
+        finish(last, halves)

@@ -178,7 +178,7 @@ def tile_picked_ccmpnormbdif_none_p_kernel(
         a_windows = [wide[last]] + wide[PACK + 1 :]
         picked, diffs, roots = {}, {}, {}
 
-        for t in range(PACK):
+        def b_side(t):
             product(
                 cb_words, cb_scales, t, z_codes, z_scales, ACT.Abs, SIXTEENTH,
                 halves[::-1] if t == 0 else whole, (5, 6) if t == 0 else ((6 + t) % 8,), (b_windows[t],),
@@ -190,13 +190,14 @@ def tile_picked_ccmpnormbdif_none_p_kernel(
             window, plain = a_windows[t], a_windows[t + 1][:, S:]
             product(
                 ca_words, ca_scales, t, z_codes, z_scales, ACT.Copy, SIXTEENTH, whole,
-                (2 + t % 3,), (window, plain),
+                (2 + t % 3,), (window,),
             )
+            nc.sync.dma_start(plain, window[:, :S])
             diffs[t] = held.tile([P, S], F32, name="diff%d" % t)
             fetch(diffs[t], window, plain, n2_list, ALU.subtract, whole)
 
         def root(t):
-            total = bank(5 + t % 2)
+            total = bank((5 + t) % 8)
             terms = [(src, cols) for src in (b_windows[t], picked[t]) for cols in blocks]
             for i, (src, cols) in enumerate(terms):
                 nc.tensor.matmul(
@@ -205,7 +206,7 @@ def tile_picked_ccmpnormbdif_none_p_kernel(
                 )
             turned = held.tile([P, S], F32, name="turned%d" % t)
             nc.scalar.activation(turned[:], total[:], ACT.Abs_reciprocal_sqrt, bias=0.5)
-            roots[t] = bank((7 + t % 2) % 8)
+            roots[t] = bank((1, 3, 4, 2)[t])
             for cols in blocks:
                 nc.tensor.transpose(roots[t][:, cols], turned[:, cols], identity[:])
 
@@ -217,9 +218,13 @@ def tile_picked_ccmpnormbdif_none_p_kernel(
                 nc.vector.tensor_tensor(result[:, cols], diffs[t][:, cols], recip[:, cols], ALU.mult)
                 nc.sync.dma_start(out_rows[t][:, :, cols], result[:, cols])
 
+        b_side(0)
         for t in range(PACK):
+            if t < last:
+                b_side(t + 1)
             a_side(t)
-            root(t)
-            if t > 0:
-                finish(t - 1, whole)
-        finish(last, halves)
+        root(0)
+        for t in range(PACK):
+            if t < last:
+                root(t + 1)
+            finish(t, halves if t >= 2 else whole)

from contextlib import ExitStack

import concourse.mybir as mybir
from concourse.masks import make_identity

K, T, S, H, C = 512, 2048, 512, 512, 512
FLOPS = 2 * K * H * S + 2 * 2 * K * C * S

F32 = mybir.dt.float32
BF16 = mybir.dt.bfloat16
I32 = mybir.dt.int32
U32 = mybir.dt.uint32
U16 = mybir.dt.uint16
U8 = mybir.dt.uint8
FP8X4 = mybir.dt.float8_e4m3fn_x4
ACT = mybir.ActivationFunctionType
ALU = mybir.AluOpType

P = 128
PACK = 4
HALF = S // 2
RUN = 8
SIXTEENTH = 0.0625


def tile_picked_ccmpnormbdif_none_p_kernel(
    tc, x_words, x_scales, w1, gs, offs, n1, ca, cb, n2, n3, out
):
    nc = tc.nc
    with ExitStack() as ctx:
        held = ctx.enter_context(tc.tile_pool(name="held", bufs=1))
        psum = ctx.enter_context(tc.psum_pool(name="psum", bufs=1))

        def load_list(name, src):
            tile = held.tile([P, S // 16], U16, name=name)
            nc.sync.dma_start(tile[:], src)
            return tile

        table_scales = held.tile([P, T], U8, name="table_scales", align_bytes=64)
        nc.vector.memset(table_scales[:].bitcast(I32), 0)
        for q in range(4):
            nc.sync.dma_start(
                table_scales[32 * q : 32 * q + 4, :].bitcast(I32),
                x_scales[0, 4 * q : 4 * q + 4, :].bitcast(I32),
            )
        warm_in = held.tile([P, 1], F32, name="warm_in")
        warm_out = held.tile([P, 1], F32, name="warm_out")
        nc.vector.memset(warm_in[:], 1.0)
        nc.scalar.activation(warm_out[:], warm_in[:], ACT.Abs_reciprocal_sqrt, bias=0.5)
        offs_list = load_list("offs_list", offs)
        cb_list = load_list("cb_list", cb)
        ca_list = load_list("ca_list", ca)
        w_rows = w1.rearrange("(p j) h -> p j h", j=PACK)
        w_raw = []
        for u in range(2):
            part = held.tile([P, PACK, H // 2], F32, name="w_raw%d" % u)
            nc.sync.dma_start(part[:], w_rows[:, :, u * (H // 2) : (u + 1) * (H // 2)])
            w_raw.append(part)
        table_words = held.tile([P, T], U32, name="table_words", align_bytes=64)
        nc.sync.dma_start(
            table_words[:].bitcast(I32),
            x_words[0].rearrange("p n t -> p (n t)").bitcast(I32),
        )
        n1_list = load_list("n1_list", n1)
        gain = held.tile([P, PACK], F32, name="gain")
        nc.sync.dma_start(gain[:], gs.rearrange("(p t) o -> p (t o)", t=PACK))
        n3_list = load_list("n3_list", n3)
        n2_list = load_list("n2_list", n2)

        identity = held.tile([P, P], F32, name="identity")
        nc.vector.memset(identity[:], 0.0)
        make_identity(nc, identity[:], nomemset=True)
        wide = [held.tile([P, 2 * S], F32, name="wide%d" % i) for i in range(2 * PACK + 1)]
        nc.vector.memset(wide[0][:, S:], 0.0)

        pair_raw = held.tile([P, 2 * C], U8, name="pair_raw", align_bytes=64)
        nc.vector.tensor_copy(pair_raw[:, :C], table_scales[:].indirect(cb_list[:]))
        nc.vector.tensor_copy(pair_raw[:, C:], table_scales[:].indirect(ca_list[:]))
        tok_scales = held.tile([P, S], U8, name="tok_scales", align_bytes=64)
        nc.vector.tensor_copy(tok_scales[:], table_scales[:].indirect(offs_list[:]))
        pair_scales = held.tile([P, 2 * C], U8, name="pair_scales", align_bytes=64)
        nc.vector.tensor_copy(
            pair_scales[:].bitcast(I32).rearrange("p (l t q w) -> p l t q w", l=2, t=PACK, w=RUN // 4),
            pair_raw[:].bitcast(I32).rearrange("p (l q t w) -> p l t q w", l=2, t=PACK, w=RUN // 4),
        )
        cb_scales, ca_scales = pair_scales[:, :C], pair_scales[:, C:]

        def pick_words(name, lst, tag):
            dealt = held.tile([P, C], U32, name=name, tag=tag, align_bytes=64)
            nc.vector.tensor_copy(
                dealt[:].rearrange("p (t q r) -> p q t r", t=PACK, r=RUN),
                table_words[:].indirect(lst[:]),
            )
            return dealt

        w_bf = held.tile([P, PACK, P, PACK], BF16, name="w_bf", align_bytes=64)
        for u in range(2):
            nc.scalar.copy(
                w_bf[:, :, u * 64 : (u + 1) * 64, :].rearrange("p t m j -> p m j t"),
                w_raw[u][:].rearrange("p j (m t) -> p m j t", t=PACK),
            )
        w_codes = held.tile([P, H], U32, name="w_codes", align_bytes=64)
        w_scales = held.tile([P, H], U8, name="w_scales", align_bytes=64)
        nc.vector.quantize_mx(
            out=w_codes[:].bitcast(FP8X4),
            scales=w_scales[:],
            in_=w_bf[:].rearrange("p t m j -> p (t m j)"),
        )

        halves = [slice(0, HALF), slice(HALF, S)]
        whole = [slice(0, S)]
        tok_words = held.tile([P, S], U32, name="tok_words", align_bytes=64)
        for cols in halves:
            nc.vector.tensor_copy(
                tok_words[:, cols],
                table_words[:].indirect(offs_list[:, cols.start // 16 : cols.stop // 16]),
            )
        cb_words = pick_words("cb_words", cb_list, "cb_words")

        def bank(n, width=S):
            return psum.tile([P, width], F32, name="bank%d" % n)

        def product(codes, scales, t, rhs, rhs_scale, func, scale, pieces, banks, copies):
            rows = slice(t * P, (t + 1) * P)
            for cols, n in zip(pieces, banks):
                acc = bank(n, cols.stop - cols.start)
                nc.tensor.matmul_mx(
                    out=acc[:],
                    lhsT=codes[:, rows].bitcast(FP8X4),
                    lhsT_scale=scales[:, rows],
                    rhs=rhs[:, cols].bitcast(FP8X4),
                    rhs_scale=rhs_scale[:, cols],
                    start=True,
                    stop=True,
                )
                for dst in copies:
                    nc.scalar.activation(dst[:, cols], acc[:], func, scale=scale)

        def fetch(dst, window, plain, lst, op, pieces):
            for cols in pieces:
                nc.vector.tensor_tensor(
                    dst[:, cols],
                    window[:].indirect(lst[:, cols.start // 16 : cols.stop // 16]),
                    plain[:, cols],
                    op,
                )

        last = PACK - 1
        neg_z = held.tile([P, PACK, S], F32, name="neg_z", tag="neg_z", align_bytes=64)
        for t in range(PACK):
            window, plain = wide[t], wide[t + 1][:, S:]
            product(
                w_codes, w_scales, t, tok_words, tok_scales, ACT.Copy, gain[:, t : t + 1],
                halves if t == 0 else whole, (0, 1) if t == 0 else (t + 1,), (window, plain),
            )
            fetch(neg_z[:, t, :], window, plain, n1_list, ALU.subtract, halves if t == last else whole)

        z_codes = held.tile([P, S], U32, name="z_codes", align_bytes=64)
        z_scales = held.tile([P, S], U8, name="z_scales", align_bytes=64)
        z_bf = [held.tile([P, HALF * PACK], BF16, name="z_bf%d" % h, align_bytes=64) for h in range(2)]
        for h, copy in ((0, nc.scalar.copy), (1, nc.vector.tensor_copy)):
            copy(
                z_bf[h][:].rearrange("p (c i t) -> p c t i", i=4, t=PACK),
                neg_z[:, :, halves[h]].rearrange("p t (c i) -> p c t i", i=4),
            )
        for h in (1, 0):
            nc.vector.quantize_mx(
                out=z_codes[:, halves[h]].bitcast(FP8X4),
                scales=z_scales[:, halves[h]],
                in_=z_bf[h][:],
            )

        ca_words = pick_words("ca_words", ca_list, "neg_z")

        out_rows = out.rearrange("(q t r) j -> t q r j", t=PACK, r=RUN)
        blocks = [slice(c * P, (c + 1) * P) for c in range(S // P)]
        b_windows = [wide[(t + PACK) % (PACK + 1)] for t in range(PACK)]
        a_windows = [wide[last]] + wide[PACK + 1 :]
        picked, diffs, roots = {}, {}, {}

        def b_side(t):
            product(
                cb_words, cb_scales, t, z_codes, z_scales, ACT.Abs, SIXTEENTH,
                halves[::-1] if t == 0 else whole, (5, 6) if t == 0 else ((6 + t) % 8,), (b_windows[t],),
            )
            picked[t] = held.tile([P, S], F32, name="picked%d" % t)
            nc.vector.tensor_copy(picked[t][:], b_windows[t][:].indirect(n3_list[:]))

        def a_side(t):
            window, plain = a_windows[t], a_windows[t + 1][:, S:]
            product(
                ca_words, ca_scales, t, z_codes, z_scales, ACT.Copy, SIXTEENTH, whole,
                (2 + t % 3,), (window,),
            )
            nc.sync.dma_start(plain, window[:, :S])
            diffs[t] = held.tile([P, S], F32, name="diff%d" % t)
            fetch(diffs[t], window, plain, n2_list, ALU.subtract, whole)

        def root(t):
            total = bank((5 + t) % 8)
            terms = [(src, cols) for src in (b_windows[t], picked[t]) for cols in blocks]
            for i, (src, cols) in enumerate(terms):
                nc.tensor.matmul(
                    total[:, cols], src[:, cols], identity[:],
                    start=(i == 0), stop=(i == len(terms) - 1), is_transpose=True,
                )
            turned = held.tile([P, S], F32, name="turned%d" % t)
            nc.scalar.activation(turned[:], total[:], ACT.Abs_reciprocal_sqrt, bias=0.5)
            roots[t] = bank((1, 3, 4, 2)[t])
            for cols in blocks:
                nc.tensor.transpose(roots[t][:, cols], turned[:, cols], identity[:])

        def finish(t, pieces):
            recip = held.tile([P, S], F32, name="recip%d" % t)
            result = held.tile([P, S], F32, name="result%d" % t)
            nc.scalar.activation(recip[:], roots[t][:], ACT.Square)
            for cols in pieces:
                nc.vector.tensor_tensor(result[:, cols], diffs[t][:, cols], recip[:, cols], ALU.mult)
                nc.sync.dma_start(out_rows[t][:, :, cols], result[:, cols])

        b_side(0)
        for t in range(PACK):
            if t < last:
                b_side(t + 1)
            a_side(t)
        root(0)
        for t in range(PACK):
            if t < last:
                root(t + 1)
            finish(t, halves if t >= 2 else whole)
